import numpy as np
import ml_dtypes


def mxq(x, axis, fmt="e4m3"):
    dtype, down = {"e4m3": (ml_dtypes.float8_e4m3fn, 7), "e5m2": (ml_dtypes.float8_e5m2, 14)}[fmt]
    v = np.moveaxis(np.asarray(x, np.float32).astype(ml_dtypes.bfloat16).astype(np.float64), axis, -1)
    blocks = v.reshape(v.shape[:-1] + (-1, 32))
    amax = np.abs(blocks).max(-1, keepdims=True)
    byte = np.maximum(np.where(amax > 0, np.frexp(amax)[1] - 1 + 127, 0) - down, 1)
    scale = np.exp2(byte - 127.0)
    codes = (blocks / scale).astype(np.float32).astype(dtype).astype(np.float64)
    return np.moveaxis((codes * scale).reshape(v.shape), -1, axis)


WIDE = False


def mx_kscale(k):
    if not WIDE:
        return np.ones(k)
    levels = np.array([10, -10, 5, -5, 0])
    if k % 512:
        return np.exp2(np.random.permutation(np.resize(levels, k // 32))).repeat(32)
    a = np.empty((k // 512, 16))
    for p in range(k // 512):
        a[p, :8] = np.random.permutation(np.resize(levels, 8))
        for g in range(8):
            far = levels[np.abs(levels - a[p, g]) >= 10]
            a[p, g + 8] = far[np.random.randint(len(far))]
    return np.exp2(a.ravel()).repeat(32)


def f64(x):
    return np.asarray(x).astype(np.float64)


def striped(idx):
    return np.tile(np.asarray(idx).reshape(-1, 16).T, (8, 1)).astype(np.uint16)


def unstriped(offs):
    return offs[:16].T.reshape(-1).astype(np.int64)


E2M1 = np.array([0.0, 0.5, 1.0, 1.5, 2.0, 3.0, 4.0, 6.0, -0.0, -0.5, -1.0, -1.5, -2.0, -3.0, -4.0, -6.0])


def pack_weight(w, fmt):
    k, n = w.shape
    w = f64(np.asarray(w, np.float32).astype(ml_dtypes.bfloat16)).reshape(k // 32, 32, n)
    amax = np.abs(w).max(1)
    if fmt == "e4m3":
        byte = np.frexp(amax)[1] - 1 + 127 - 7
    else:
        mant, ex = np.frexp(amax / 6.0)
        byte = np.where(mant > 0.5, ex, ex - 1) + 127
    byte = np.clip(np.where(amax > 0, byte, 1), 1, 254)
    scaled = (w * np.exp2(127.0 - byte)[:, None, :]).reshape(k, n).astype(np.float32)
    by_word = np.ascontiguousarray(scaled.reshape(k // 512, 128, 4, n).transpose(0, 1, 3, 2))
    if fmt == "e4m3":
        words = by_word.astype(ml_dtypes.float8_e4m3fn).view(np.uint8)
    else:
        c = by_word.astype(ml_dtypes.float4_e2m1fn).view(np.uint8) & 0xF
        words = (c[..., 0::2] | (c[..., 1::2] << 4)).reshape(k // 512, 128, 2 * n)
    return np.ascontiguousarray(words), np.ascontiguousarray(byte.astype(np.uint8).reshape(k // 512, 16, n))


def unpack_weight(words, scales, fmt):
    g, _, n = scales.shape
    words = np.ascontiguousarray(words).reshape(g, 128, n, -1)
    if fmt == "e4m3":
        vals = words.view(ml_dtypes.float8_e4m3fn).astype(np.float64)
    else:
        nib = np.empty((g, 128, n, 4), np.uint8)
        nib[..., 0::2] = words & 0xF
        nib[..., 1::2] = words >> 4
        vals = E2M1[nib]
    vals = vals * np.repeat(np.exp2(scales.astype(np.float64) - 127.0), 8, axis=1)[..., None]
    return vals.transpose(0, 1, 3, 2).reshape(g * 512, n)


def bf(x):
    return np.asarray(x, np.float32).astype(ml_dtypes.bfloat16)


def planes(Y):
    r, m = Y.shape
    b = f64(bf(Y)).reshape(r // 32, 32, m)
    amax = np.abs(b).max(1)
    byte = np.clip(np.where(amax > 0, np.frexp(amax)[1] - 1 + 127 - 7, 1), 1, 254)
    codes = (b * np.exp2(127.0 - byte)[:, None, :]).reshape(r, m).astype(np.float32).astype(ml_dtypes.float8_e4m3fn).view(np.uint8)
    words = codes.reshape(r // 512, 128, 4, m).transpose(0, 1, 3, 2)
    return np.ascontiguousarray(words), np.ascontiguousarray(byte.astype(np.uint8).reshape(r // 512, 16, m))


D, E, T, I, Q = 512, 512, 2048, 512, 256


def setup_inputs():
    n = np.random.standard_normal
    idx2 = np.random.permutation(I)[:I]
    idx = np.random.permutation(T)[:I]
    fd = mx_kscale(D)
    fi = mx_kscale(I)
    ti = np.ones(T)
    ti[idx] = fi
    keysp = pack_weight(n((D, T)) / fd[:, None], "e4m3")
    return {
        "query": (n((D, Q)) * 0.7 / np.sqrt(D) * fd[:, None]).astype(np.float32),
        "keys_words": keysp[0],
        "keys_scales": keysp[1],
        "os": (np.random.uniform(4.0, 16.0, (1, I)) * fi).astype(np.float32),
        "vals": (n((E, T)) / ti).astype(np.float32),
        "offs2": striped(idx2),
        "offs": striped(idx),
    }


def reference(query, keys_words, keys_scales, os, vals, offs2, offs):
    idx2 = unstriped(offs2)
    idx = unstriped(offs)
    keysu = unpack_weight(keys_words, keys_scales, "e4m3")
    queryq = mxq(f64(query), 0, "e4m3")
    keysidxg = keysu[:, idx]
    a = queryq.T @ keysidxg
    pa = np.exp(a)
    pb = np.sqrt(pa)
    p = pa * pb[:, idx2]
    z = np.sum(p, axis=1, keepdims=True)
    w = p / z
    wo1 = w * f64(os)
    wt1 = wo1.T
    vt1 = f64(vals)[:, idx].T
    vt1q = mxq(vt1, 0, "e4m3")
    wt1q = mxq(wt1, 0, "e4m3")
    o = vt1q.T @ wt1q
    words, scales = planes(o)
    return o, words, scales

@@ -1,0 +1,206 @@
+from contextlib import ExitStack
+
+import concourse.mybir as mybir
+from concourse.masks import make_identity
+
+D, E, T, I, Q = 512, 512, 2048, 512, 256
+FLOPS = 2 * Q * I * D + 2 * E * Q * I
+
+F32 = mybir.dt.float32
+BF16 = mybir.dt.bfloat16
+I32 = mybir.dt.int32
+U32 = mybir.dt.uint32
+U16 = mybir.dt.uint16
+U8 = mybir.dt.uint8
+FP8X4 = mybir.dt.float8_e4m3fn_x4
+ALU = mybir.AluOpType
+ACT = mybir.ActivationFunctionType
+
+P = 128
+PACK = 4
+HALVES = Q // P
+SPARE = 16
+CAST_PLANE = 1
+
+
+def tile_attend_linkedproduct_pl_kernel(tc, query, keys_words, keys_scales, slot_factor, vals, offs2, offs, out_0, out_1, out_2):
+    nc = tc.nc
+    with ExitStack() as ctx:
+        sb = ctx.enter_context(tc.tile_pool(name="sb", bufs=1))
+        ps = ctx.enter_context(tc.psum_pool(name="ps", bufs=1))
+
+        def tile(shape, dtype, name, tag=None):
+            return sb.tile(shape, dtype, name=name, tag=tag or name, align_bytes=64)
+
+        slot_list = tile([P, I // 16], U16, "slot_list")
+        link_list = tile([P, I // 16], U16, "link_list")
+        key_scales = tile([P, T], U8, "key_scales")
+        key_words = tile([P, T], I32, "key_words")
+        q_raw = tile([P, PACK, Q], F32, "q_raw")
+        os_cols = tile([P, PACK], F32, "os_cols")
+        v_raw = {t: tile([P, T], F32, f"v_raw{t}") for t in range(PACK) if t != CAST_PLANE}
+        v_half = [tile([P, T // 2], F32, f"v_half{h}") for h in range(2)]
+
+        scale_words = key_scales[:].bitcast(I32)
+        nc.vector.memset(scale_words, 0)
+        v_planes = vals.rearrange("(p t) n -> t p n", t=PACK)
+        nc.sync.dma_start(slot_list[:], offs)
+        nc.sync.dma_start(key_words[:], keys_words[0].rearrange("p n r -> p (n r)").bitcast(I32))
+        for quad in range(4):
+            nc.sync.dma_start(
+                key_scales[32 * quad : 32 * quad + 4, :].bitcast(I32),
+                keys_scales[0, 4 * quad : 4 * quad + 4, :].bitcast(I32),
+            )
+        nc.sync.dma_start(q_raw[:], query.rearrange("(p t) q -> p t q", t=PACK))
+        nc.sync.dma_start(v_raw[0][:], v_planes[0])
+        nc.sync.dma_start(link_list[:], offs2)
+        nc.sync.dma_start(os_cols[:], slot_factor.rearrange("o (p t) -> (o p) t", t=PACK))
+        for h in range(2):
+            nc.sync.dma_start(v_half[h][:], v_planes[CAST_PLANE][:, h * T // 2 : (h + 1) * T // 2])
+        for t in range(2, PACK):
+            nc.sync.dma_start(v_raw[t][:], v_planes[t])
+
+        ident = tile([P, P], F32, "ident")
+        make_identity(nc, ident[:])
+        zeros = tile([P, SPARE], F32, "zeros")
+        nc.gpsimd.memset(zeros[:], 0.0)
+        pb = [tile([P, I + SPARE], F32, f"pb{h}") for h in range(HALVES)]
+        for h in range(HALVES):
+            nc.scalar.activation(pb[h][:, I:], zeros[:], ACT.Exp)
+
+        kg_scales = tile([P, I], U8, "kg_scales")
+        kg_words = tile([P, I], U32, "kg_words")
+        nc.vector.tensor_copy(kg_words[:], key_words[:].bitcast(U32).indirect(slot_list[:]))
+        nc.vector.tensor_copy(kg_scales[:], key_scales[:].indirect(slot_list[:]))
+
+        q_codes, q_scales = [], []
+        for h in range(HALVES):
+            q_bf = tile([P, P, PACK], BF16, f"q_bf{h}")
+            dst = q_bf[:].rearrange("p (c i) t -> p c t i", i=4)
+            src = q_raw[:, :, h * P : (h + 1) * P].rearrange("p t (c i) -> p c t i", i=4)
+            nc.scalar.copy(dst, src)
+            codes = tile([P, P], U32, f"q_codes{h}")
+            scales = tile([P, P], U8, f"q_scales{h}")
+            nc.vector.quantize_mx(codes[:].bitcast(FP8X4), scales[:], q_bf[:].rearrange("p c t -> p (c t)"))
+            q_codes.append(codes)
+            q_scales.append(scales)
+
+        pa = []
+        for h in range(HALVES):
+            scores = ps.tile([P, I], F32, name=f"scores{h}", tag=f"scores{h}")
+            nc.tensor.matmul_mx(
+                scores[:], lhsT=q_codes[h][:].bitcast(FP8X4), lhsT_scale=q_scales[h][:],
+                rhs=kg_words[:].bitcast(FP8X4), rhs_scale=kg_scales[:], start=True, stop=True,
+            )
+            neg_half = tile([P, I], F32, f"neg_half{h}")
+            shift = tile([P, 1], F32, f"shift{h}")
+            nc.vector.tensor_scalar(neg_half[:], scores[:], -0.5, None, ALU.mult, ALU.min, accum_out=shift[:])
+            nc.scalar.activation(pb[h][:, :I], neg_half[:], ACT.Exp, bias=shift[:], scale=-1.0)
+            sq = tile([P, I], F32, f"pa{h}")
+            nc.scalar.activation(sq[:], pb[h][:, :I], ACT.Square)
+            pa.append(sq)
+
+        os_rows = ps.tile([P, PACK, P], F32, name="os_rows")
+        for t in range(PACK):
+            nc.tensor.transpose(os_rows[:, t, :], os_cols[:, t : t + 1].to_broadcast([P, P]), ident[:])
+
+        turned_a = tile([P, I], BF16, "turned_a")
+        v_pool_bf = tile([P, T], BF16, "v_pool_bf")
+        turned_b = tile([P, 4 * I], BF16, "turned_b", "v_pool_bf")
+        turned_d = tile([P, I], BF16, "turned_d")
+        vt_bf = [turned_a[:], turned_b[:, :I], turned_b[:, 2 * I : 3 * I], turned_b[:, 3 * I :]]
+        wt_bf = [turned_b[:, I : 2 * I], turned_d[:]]
+
+        def gather_values(t):
+            v_bf = tile([P, I], BF16, f"v_bf{t}")
+            if t == CAST_PLANE:
+                nc.scalar.activation(v_bf[:], v_pool_bf[:].indirect(slot_list[:]), ACT.Copy)
+            else:
+                nc.vector.tensor_copy(v_bf[:], v_raw[t][:].indirect(slot_list[:]))
+            turned = ps.tile([P, 2, P], F32, name=f"v_turned{t}", tag=f"v_turned{t % 3}")
+            pairs = v_bf[:].bitcast(F32)
+            for u in range(2):
+                nc.tensor.transpose(turned[:, u, :], pairs[:, u::2], ident[:])
+            nc.scalar.copy(
+                vt_bf[t].bitcast(F32).rearrange("p (c u) -> p c u", u=2),
+                turned[:].rearrange("p u c -> p c u"),
+            )
+
+        def quantize(flat, operands, name, tag=None):
+            codes = tile([P, operands * P], U32, f"{name}_codes", tag)
+            scales = tile([P, operands * P], U8, f"{name}_scales")
+            nc.vector.quantize_mx(codes[:].bitcast(FP8X4), scales[:], flat)
+            return [
+                (codes[:, j * P : (j + 1) * P].bitcast(FP8X4), scales[:, j * P : (j + 1) * P]) for j in range(operands)
+            ]
+
+        gather_values(0)
+
+        parts = []
+        sums = tile([P, HALVES], F32, "sums")
+        for h in range(HALVES):
+            part = tile([P, I], F32, f"part{h}")
+            nc.vector.tensor_tensor(part[:], pb[h][:].indirect(link_list[:]), pa[h][:], ALU.mult)
+            nc.scalar.activation(v_pool_bf[:, h * T // 2 : (h + 1) * T // 2], v_half[h][:], ACT.Copy)
+            summed = tile([P, I], F32, f"summed{h}", f"v_half{h}")
+            nc.scalar.activation(summed[:], part[:], ACT.Copy, accum_out=sums[:, h : h + 1])
+            parts.append(part)
+
+        gather_values(CAST_PLANE)
+
+        def weights(h, tag):
+            w_bf = tile([P, I], BF16, f"w_bf{h}", tag)
+            nc.vector.scalar_tensor_tensor(
+                w_bf[:].rearrange("p (s t) -> p s t", t=PACK), parts[h][:].rearrange("p (s t) -> p s t", t=PACK),
+                inverse[:, h : h + 1], os_rows[:].rearrange("p t s -> p s t"), ALU.mult, ALU.mult,
+            )
+            w_turned = ps.tile([P, 2, P], F32, name=f"w_turned{h}", tag=f"scores{h}")
+            pairs = w_bf[:].bitcast(F32)
+            for u in range(2):
+                nc.tensor.transpose(w_turned[:, u, :], pairs[:, u::2], ident[:])
+            nc.scalar.copy(
+                wt_bf[h].bitcast(F32).rearrange("p (c u) -> p c u", u=2),
+                w_turned[:].rearrange("p u c -> p c u"),
+            )
+
+        gather_values(2)
+        inverse = tile([P, HALVES], F32, "inverse", "v_raw2")
+        nc.vector.reciprocal(inverse[:], sums[:])
+        (v0,) = quantize(turned_a[:], 1, "mx_a", "sums")
+        weights(0, None)
+        gather_values(3)
+        weights(1, "v_raw3")
+        v1, w0 = quantize(turned_b[:, : 2 * I], 2, "mx_b", "part1")
+        v2, v3 = quantize(turned_b[:, 2 * I :], 2, "mx_c")
+        (w1,) = quantize(turned_d[:], 1, "mx_d")
+
+        out_rows = out_0.rearrange("(p t) q -> p t q", t=PACK)
+        y_codes = tile([P, Q], I32, "y_codes")
+        y_scales = tile([P, Q], U8, "y_scales")
+        for h, (w_codes, w_scales) in enumerate((w0, w1)):
+            cols = slice(h * P, (h + 1) * P)
+            result = ps.tile([P, PACK, P], F32, name=f"result{h}")
+            for t, (v_codes, v_scales) in enumerate((v0, v1, v2, v3)):
+                nc.tensor.matmul_mx(
+                    result[:, t, :], lhsT=v_codes, lhsT_scale=v_scales, rhs=w_codes, rhs_scale=w_scales,
+                    start=True, stop=True,
+                )
+            staged = tile([P, PACK, P], F32, f"staged{h}")
+            y_bf = tile([P, P, PACK], BF16, f"y_bf{h}")
+            if h == 0:
+                nc.scalar.copy(staged[:], result[:])
+                nc.vector.tensor_copy(
+                    y_bf[:].rearrange("p (c i) t -> p c t i", i=4), staged[:].rearrange("p t (c i) -> p c t i", i=4)
+                )
+                nc.sync.dma_start(out_rows[:, :, cols], staged[:])
+            else:
+                nc.scalar.copy(y_bf[:], result[:].rearrange("p t c -> p c t"))
+                nc.scalar.copy(staged[:], result[:])
+                nc.scalar.dma_start(out_rows[:, :, cols], staged[:])
+            nc.vector.quantize_mx(y_codes[:, cols].bitcast(FP8X4), y_scales[:, cols], y_bf[:].rearrange("p c t -> p (c t)"))
+        nc.sync.dma_start(out_1[0].rearrange("p c r -> p (c r)").bitcast(I32), y_codes[:])
+        for quad in range(4):
+            nc.sync.dma_start(
+                out_2[0, 4 * quad : 4 * quad + 4, :].bitcast(I32),
+                y_scales[32 * quad : 32 * quad + 4, :].bitcast(I32),
+            )

@@ -44,8 +44,8 @@ def tile_attend_linkedproduct_pl_kernel(tc, query, keys_words, keys_scales, slot
         scale_words = key_scales[:].bitcast(I32)
         nc.vector.memset(scale_words, 0)
         v_planes = vals.rearrange("(p t) n -> t p n", t=PACK)
-        nc.sync.dma_start(slot_list[:], offs)
         nc.sync.dma_start(key_words[:], keys_words[0].rearrange("p n r -> p (n r)").bitcast(I32))
+        nc.sync.dma_start(slot_list[:], offs)
         for quad in range(4):
             nc.sync.dma_start(
                 key_scales[32 * quad : 32 * quad + 4, :].bitcast(I32),
@@ -136,45 +136,51 @@ def tile_attend_linkedproduct_pl_kernel(tc, query, keys_words, keys_scales, slot
 
         gather_values(0)
 
-        parts = []
-        sums = tile([P, HALVES], F32, "sums")
+        parts, sums = [], []
         for h in range(HALVES):
             part = tile([P, I], F32, f"part{h}")
             nc.vector.tensor_tensor(part[:], pb[h][:].indirect(link_list[:]), pa[h][:], ALU.mult)
             nc.scalar.activation(v_pool_bf[:, h * T // 2 : (h + 1) * T // 2], v_half[h][:], ACT.Copy)
             summed = tile([P, I], F32, f"summed{h}", f"v_half{h}")
-            nc.scalar.activation(summed[:], part[:], ACT.Copy, accum_out=sums[:, h : h + 1])
+            z = tile([P, 1], F32, f"z{h}")
+            nc.scalar.activation(summed[:], part[:], ACT.Copy, accum_out=z[:])
+            sums.append(z)
             parts.append(part)
 
         gather_values(CAST_PLANE)
 
-        def weights(h, tag):
-            w_bf = tile([P, I], BF16, f"w_bf{h}", tag)
-            nc.vector.scalar_tensor_tensor(
-                w_bf[:].rearrange("p (s t) -> p s t", t=PACK), parts[h][:].rearrange("p (s t) -> p s t", t=PACK),
-                inverse[:, h : h + 1], os_rows[:].rearrange("p t s -> p s t"), ALU.mult, ALU.mult,
-            )
+        def inverse_sum(h, tag):
+            inverse = tile([P, 1], F32, f"inverse{h}", tag)
+            nc.vector.reciprocal(inverse[:], sums[h][:])
+            return inverse
+
+        def weights(h, inverse, tag):
+            w_bf = tile([P, 2, P, 2], BF16, f"w_bf{h}", tag)
             w_turned = ps.tile([P, 2, P], F32, name=f"w_turned{h}", tag=f"scores{h}")
-            pairs = w_bf[:].bitcast(F32)
             for u in range(2):
-                nc.tensor.transpose(w_turned[:, u, :], pairs[:, u::2], ident[:])
+                nc.vector.scalar_tensor_tensor(
+                    w_bf[:, u], parts[h][:].rearrange("p (s u e) -> p u s e", u=2, e=2)[:, u],
+                    inverse[:], os_rows[:, 2 * u : 2 * u + 2, :].rearrange("p e s -> p s e"), ALU.mult, ALU.mult,
+                )
+                nc.tensor.transpose(w_turned[:, u, :], w_bf[:, u].rearrange("p s e -> p (s e)").bitcast(F32), ident[:])
             nc.scalar.copy(
                 wt_bf[h].bitcast(F32).rearrange("p (c u) -> p c u", u=2),
                 w_turned[:].rearrange("p u c -> p c u"),
             )
 
         gather_values(2)
-        inverse = tile([P, HALVES], F32, "inverse", "v_raw2")
-        nc.vector.reciprocal(inverse[:], sums[:])
-        (v0,) = quantize(turned_a[:], 1, "mx_a", "sums")
-        weights(0, None)
+        inverse = inverse_sum(0, "v_raw2")
+        (v0,) = quantize(turned_a[:], 1, "mx_a", "z0")
+        weights(0, inverse, None)
+        inverse = inverse_sum(1, "part0")
         gather_values(3)
-        weights(1, "v_raw3")
+        weights(1, inverse, "v_raw3")
         v1, w0 = quantize(turned_b[:, : 2 * I], 2, "mx_b", "part1")
         v2, v3 = quantize(turned_b[:, 2 * I :], 2, "mx_c")
         (w1,) = quantize(turned_d[:], 1, "mx_d")
 
         out_rows = out_0.rearrange("(p t) q -> p t q", t=PACK)
+        y_bf = tile([P, Q, PACK], BF16, "y_bf")
         y_codes = tile([P, Q], I32, "y_codes")
         y_scales = tile([P, Q], U8, "y_scales")
         for h, (w_codes, w_scales) in enumerate((w0, w1)):
@@ -186,21 +192,19 @@ def tile_attend_linkedproduct_pl_kernel(tc, query, keys_words, keys_scales, slot
                     start=True, stop=True,
                 )
             staged = tile([P, PACK, P], F32, f"staged{h}")
-            y_bf = tile([P, P, PACK], BF16, f"y_bf{h}")
-            if h == 0:
-                nc.scalar.copy(staged[:], result[:])
-                nc.vector.tensor_copy(
-                    y_bf[:].rearrange("p (c i) t -> p c t i", i=4), staged[:].rearrange("p t (c i) -> p c t i", i=4)
-                )
-                nc.sync.dma_start(out_rows[:, :, cols], staged[:])
-            else:
-                nc.scalar.copy(y_bf[:], result[:].rearrange("p t c -> p c t"))
-                nc.scalar.copy(staged[:], result[:])
-                nc.scalar.dma_start(out_rows[:, :, cols], staged[:])
-            nc.vector.quantize_mx(y_codes[:, cols].bitcast(FP8X4), y_scales[:, cols], y_bf[:].rearrange("p c t -> p (c t)"))
+            nc.scalar.copy(staged[:], result[:])
+            (nc.sync, nc.scalar)[h].dma_start(out_rows[:, :, cols], staged[:])
+            nc.vector.tensor_copy(
+                y_bf[:, cols, :].rearrange("p (c i) t -> p c t i", i=4), staged[:].rearrange("p t (c i) -> p c t i", i=4)
+            )
+        for h in range(HALVES):
+            cols = slice(h * P, (h + 1) * P)
+            nc.vector.quantize_mx(
+                y_codes[:, cols].bitcast(FP8X4), y_scales[:, cols], y_bf[:, cols, :].rearrange("p c t -> p (c t)")
+            )
         nc.sync.dma_start(out_1[0].rearrange("p c r -> p (c r)").bitcast(I32), y_codes[:])
         for quad in range(4):
-            nc.sync.dma_start(
+            (nc.scalar, nc.sync)[quad % 2].dma_start(
                 out_2[0, 4 * quad : 4 * quad + 4, :].bitcast(I32),
                 y_scales[32 * quad : 32 * quad + 4, :].bitcast(I32),
             )

@@ -46,11 +46,8 @@ def tile_attend_linkedproduct_pl_kernel(tc, query, keys_words, keys_scales, slot
         v_planes = vals.rearrange("(p t) n -> t p n", t=PACK)
         nc.sync.dma_start(key_words[:], keys_words[0].rearrange("p n r -> p (n r)").bitcast(I32))
         nc.sync.dma_start(slot_list[:], offs)
-        for quad in range(4):
-            nc.sync.dma_start(
-                key_scales[32 * quad : 32 * quad + 4, :].bitcast(I32),
-                keys_scales[0, 4 * quad : 4 * quad + 4, :].bitcast(I32),
-            )
+        for r in range(4):
+            nc.sync.dma_start(scale_words[r:P:32, :], keys_scales[0].bitcast(I32)[r:16:4, :])
         nc.sync.dma_start(q_raw[:], query.rearrange("(p t) q -> p t q", t=PACK))
         nc.sync.dma_start(v_raw[0][:], v_planes[0])
         nc.sync.dma_start(link_list[:], offs2)
@@ -185,14 +182,15 @@ def tile_attend_linkedproduct_pl_kernel(tc, query, keys_words, keys_scales, slot
         y_scales = tile([P, Q], U8, "y_scales")
         for h, (w_codes, w_scales) in enumerate((w0, w1)):
             cols = slice(h * P, (h + 1) * P)
-            result = ps.tile([P, PACK, P], F32, name=f"result{h}")
-            for t, (v_codes, v_scales) in enumerate((v0, v1, v2, v3)):
-                nc.tensor.matmul_mx(
-                    result[:, t, :], lhsT=v_codes, lhsT_scale=v_scales, rhs=w_codes, rhs_scale=w_scales,
-                    start=True, stop=True,
-                )
             staged = tile([P, PACK, P], F32, f"staged{h}")
-            nc.scalar.copy(staged[:], result[:])
+            for j, pair in enumerate(((v0, v1), (v2, v3))):
+                result = ps.tile([P, 2, P], F32, name=f"result{h}_{j}", tag=(f"result{h}", f"v_turned{h + 1}")[j])
+                for t, (v_codes, v_scales) in enumerate(pair):
+                    nc.tensor.matmul_mx(
+                        result[:, t, :], lhsT=v_codes, lhsT_scale=v_scales, rhs=w_codes, rhs_scale=w_scales,
+                        start=True, stop=True,
+                    )
+                nc.scalar.copy(staged[:, 2 * j : 2 * j + 2, :], result[:])
             (nc.sync, nc.scalar)[h].dma_start(out_rows[:, :, cols], staged[:])
             nc.vector.tensor_copy(
                 y_bf[:, cols, :].rearrange("p (c i) t -> p c t i", i=4), staged[:].rearrange("p t (c i) -> p c t i", i=4)

@@ -20,10 +20,12 @@ P = 128
 PACK = 4
 HALVES = Q // P
 SPARE = 16
-CAST_PLANE = 1
+CAST_CUTS = (0, 768, 1408, T)
 
 
-def tile_attend_linkedproduct_pl_kernel(tc, query, keys_words, keys_scales, slot_factor, vals, offs2, offs, out_0, out_1, out_2):
+def tile_attend_linkedproduct_pl_kernel(
+    tc, query, keys_words, keys_scales, slot_factor, vals, offs2, offs, out_0, out_1, out_2
+):
     nc = tc.nc
     with ExitStack() as ctx:
         sb = ctx.enter_context(tc.tile_pool(name="sb", bufs=1))
@@ -32,14 +34,18 @@ def tile_attend_linkedproduct_pl_kernel(tc, query, keys_words, keys_scales, slot
         def tile(shape, dtype, name, tag=None):
             return sb.tile(shape, dtype, name=name, tag=tag or name, align_bytes=64)
 
+        def bank(shape, name, tag=None):
+            return ps.tile(shape, F32, name=name, tag=tag or name)
+
         slot_list = tile([P, I // 16], U16, "slot_list")
         link_list = tile([P, I // 16], U16, "link_list")
         key_scales = tile([P, T], U8, "key_scales")
         key_words = tile([P, T], I32, "key_words")
         q_raw = tile([P, PACK, Q], F32, "q_raw")
-        os_cols = tile([P, PACK], F32, "os_cols")
-        v_raw = {t: tile([P, T], F32, f"v_raw{t}") for t in range(PACK) if t != CAST_PLANE}
-        v_half = [tile([P, T // 2], F32, f"v_half{h}") for h in range(2)]
+        factor_cols = tile([P, PACK], F32, "factor_cols")
+        v_raw = {t: tile([P, T], F32, f"v_raw{t}") for t in (0, 2, 3)}
+        pieces = [slice(CAST_CUTS[j], CAST_CUTS[j + 1]) for j in range(3)]
+        v_piece = [tile([P, cols.stop - cols.start], F32, f"v_piece{j}") for j, cols in enumerate(pieces)]
 
         scale_words = key_scales[:].bitcast(I32)
         nc.vector.memset(scale_words, 0)
@@ -49,157 +55,174 @@ def tile_attend_linkedproduct_pl_kernel(tc, query, keys_words, keys_scales, slot
         for r in range(4):
             nc.sync.dma_start(scale_words[r:P:32, :], keys_scales[0].bitcast(I32)[r:16:4, :])
         nc.sync.dma_start(q_raw[:], query.rearrange("(p t) q -> p t q", t=PACK))
+        nc.sync.dma_start(v_piece[0][:], v_planes[1][:, pieces[0]])
         nc.sync.dma_start(v_raw[0][:], v_planes[0])
         nc.sync.dma_start(link_list[:], offs2)
-        nc.sync.dma_start(os_cols[:], slot_factor.rearrange("o (p t) -> (o p) t", t=PACK))
-        for h in range(2):
-            nc.sync.dma_start(v_half[h][:], v_planes[CAST_PLANE][:, h * T // 2 : (h + 1) * T // 2])
-        for t in range(2, PACK):
-            nc.sync.dma_start(v_raw[t][:], v_planes[t])
+        nc.sync.dma_start(factor_cols[:], slot_factor.rearrange("o (p t) -> (o p) t", t=PACK))
+        nc.sync.dma_start(v_piece[1][:], v_planes[1][:, pieces[1]])
+        nc.sync.dma_start(v_raw[2][:], v_planes[2])
+        nc.sync.dma_start(v_piece[2][:], v_planes[1][:, pieces[2]])
+        nc.sync.dma_start(v_raw[3][:], v_planes[3])
 
         ident = tile([P, P], F32, "ident")
         make_identity(nc, ident[:])
         zeros = tile([P, SPARE], F32, "zeros")
         nc.gpsimd.memset(zeros[:], 0.0)
-        pb = [tile([P, I + SPARE], F32, f"pb{h}") for h in range(HALVES)]
+        roots = [tile([P, I + SPARE], F32, f"roots{h}") for h in range(HALVES)]
         for h in range(HALVES):
-            nc.scalar.activation(pb[h][:, I:], zeros[:], ACT.Exp)
+            nc.scalar.activation(roots[h][:, I:], zeros[:], ACT.Exp)
 
-        kg_scales = tile([P, I], U8, "kg_scales")
-        kg_words = tile([P, I], U32, "kg_words")
-        nc.vector.tensor_copy(kg_words[:], key_words[:].bitcast(U32).indirect(slot_list[:]))
-        nc.vector.tensor_copy(kg_scales[:], key_scales[:].indirect(slot_list[:]))
+        listed_words = tile([P, I], U32, "listed_words")
+        listed_scales = tile([P, I], U8, "listed_scales")
+        nc.vector.tensor_copy(listed_words[:], key_words[:].bitcast(U32).indirect(slot_list[:]))
+        nc.vector.tensor_copy(listed_scales[:], key_scales[:].indirect(slot_list[:]))
 
-        q_codes, q_scales = [], []
+        def quantize(codes, scales, values):
+            nc.vector.quantize_mx(codes.bitcast(FP8X4), scales, values)
+
+        def interleave(copy, side_by_side, planes):
+            copy(
+                side_by_side.rearrange("p (c i t) -> p c t i", i=4, t=PACK),
+                planes.rearrange("p t (c i) -> p c t i", i=4),
+            )
+
+        q_codes = tile([P, Q], U32, "q_codes")
+        q_scales = tile([P, Q], U8, "q_scales")
+        halves = [slice(h * P, (h + 1) * P) for h in range(HALVES)]
         for h in range(HALVES):
-            q_bf = tile([P, P, PACK], BF16, f"q_bf{h}")
-            dst = q_bf[:].rearrange("p (c i) t -> p c t i", i=4)
-            src = q_raw[:, :, h * P : (h + 1) * P].rearrange("p t (c i) -> p c t i", i=4)
-            nc.scalar.copy(dst, src)
-            codes = tile([P, P], U32, f"q_codes{h}")
-            scales = tile([P, P], U8, f"q_scales{h}")
-            nc.vector.quantize_mx(codes[:].bitcast(FP8X4), scales[:], q_bf[:].rearrange("p c t -> p (c t)"))
-            q_codes.append(codes)
-            q_scales.append(scales)
+            q_bf = tile([P, P * PACK], BF16, f"q_bf{h}")
+            interleave(nc.scalar.copy, q_bf[:], q_raw[:, :, halves[h]])
+            quantize(q_codes[:, halves[h]], q_scales[:, halves[h]], q_bf[:])
 
-        pa = []
+        v1_bf = tile([P, T], BF16, "v1_bf")
+
+        def cast_piece(j):
+            nc.scalar.activation(v1_bf[:, pieces[j]], v_piece[j][:], ACT.Copy)
+
+        cast_piece(0)
+
+        exps = []
         for h in range(HALVES):
-            scores = ps.tile([P, I], F32, name=f"scores{h}", tag=f"scores{h}")
+            scores = bank([P, I], f"scores{h}")
             nc.tensor.matmul_mx(
-                scores[:], lhsT=q_codes[h][:].bitcast(FP8X4), lhsT_scale=q_scales[h][:],
-                rhs=kg_words[:].bitcast(FP8X4), rhs_scale=kg_scales[:], start=True, stop=True,
+                scores[:], lhsT=q_codes[:, halves[h]].bitcast(FP8X4), lhsT_scale=q_scales[:, halves[h]],
+                rhs=listed_words[:].bitcast(FP8X4), rhs_scale=listed_scales[:], start=True, stop=True,
             )
             neg_half = tile([P, I], F32, f"neg_half{h}")
             shift = tile([P, 1], F32, f"shift{h}")
             nc.vector.tensor_scalar(neg_half[:], scores[:], -0.5, None, ALU.mult, ALU.min, accum_out=shift[:])
-            nc.scalar.activation(pb[h][:, :I], neg_half[:], ACT.Exp, bias=shift[:], scale=-1.0)
-            sq = tile([P, I], F32, f"pa{h}")
-            nc.scalar.activation(sq[:], pb[h][:, :I], ACT.Square)
-            pa.append(sq)
+            nc.scalar.activation(roots[h][:, :I], neg_half[:], ACT.Exp, bias=shift[:], scale=-1.0)
+            exp_h = tile([P, I], F32, f"exps{h}")
+            nc.scalar.activation(exp_h[:], roots[h][:, :I], ACT.Square)
+            exps.append(exp_h)
 
-        os_rows = ps.tile([P, PACK, P], F32, name="os_rows")
+        factor_rows = bank([P, PACK, P], "factor_rows")
         for t in range(PACK):
-            nc.tensor.transpose(os_rows[:, t, :], os_cols[:, t : t + 1].to_broadcast([P, P]), ident[:])
+            nc.tensor.transpose(factor_rows[:, t, :], factor_cols[:, t : t + 1].to_broadcast([P, P]), ident[:])
 
-        turned_a = tile([P, I], BF16, "turned_a")
-        v_pool_bf = tile([P, T], BF16, "v_pool_bf")
-        turned_b = tile([P, 4 * I], BF16, "turned_b", "v_pool_bf")
-        turned_d = tile([P, I], BF16, "turned_d")
-        vt_bf = [turned_a[:], turned_b[:, :I], turned_b[:, 2 * I : 3 * I], turned_b[:, 3 * I :]]
-        wt_bf = [turned_b[:, I : 2 * I], turned_d[:]]
-
-        def gather_values(t):
-            v_bf = tile([P, I], BF16, f"v_bf{t}")
-            if t == CAST_PLANE:
-                nc.scalar.activation(v_bf[:], v_pool_bf[:].indirect(slot_list[:]), ACT.Copy)
-            else:
-                nc.vector.tensor_copy(v_bf[:], v_raw[t][:].indirect(slot_list[:]))
-            turned = ps.tile([P, 2, P], F32, name=f"v_turned{t}", tag=f"v_turned{t % 3}")
-            pairs = v_bf[:].bitcast(F32)
-            for u in range(2):
-                nc.tensor.transpose(turned[:, u, :], pairs[:, u::2], ident[:])
+        def copy_turned(side_by_side, turned):
             nc.scalar.copy(
-                vt_bf[t].bitcast(F32).rearrange("p (c u) -> p c u", u=2),
-                turned[:].rearrange("p u c -> p c u"),
+                side_by_side.bitcast(F32).rearrange("p (c u) -> p c u", u=2), turned[:].rearrange("p u c -> p c u")
             )
 
-        def quantize(flat, operands, name, tag=None):
-            codes = tile([P, operands * P], U32, f"{name}_codes", tag)
-            scales = tile([P, operands * P], U8, f"{name}_scales")
-            nc.vector.quantize_mx(codes[:].bitcast(FP8X4), scales[:], flat)
-            return [
-                (codes[:, j * P : (j + 1) * P].bitcast(FP8X4), scales[:, j * P : (j + 1) * P]) for j in range(operands)
-            ]
+        def gather_values(t):
+            listed = tile([P, I], BF16, f"listed_v{t}")
+            if t == 1:
+                nc.scalar.activation(listed[:], v1_bf[:].indirect(slot_list[:]), ACT.Copy)
+            else:
+                nc.vector.tensor_copy(listed[:], v_raw[t][:].indirect(slot_list[:]))
+            return listed
 
-        gather_values(0)
+        def turn_values(t, listed, side_by_side):
+            turned = bank([P, 2, P], f"v_turned{t}", f"v_turned{t % 3}")
+            pairs = listed[:].bitcast(F32)
+            for u in range(2):
+                nc.tensor.transpose(turned[:, u, :], pairs[:, u::2], ident[:])
+            copy_turned(side_by_side, turned)
 
-        parts, sums = [], []
+        v0_turned = tile([P, I], BF16, "v0_turned")
+        turn_values(0, gather_values(0), v0_turned[:])
+
+        parts = []
         for h in range(HALVES):
             part = tile([P, I], F32, f"part{h}")
-            nc.vector.tensor_tensor(part[:], pb[h][:].indirect(link_list[:]), pa[h][:], ALU.mult)
-            nc.scalar.activation(v_pool_bf[:, h * T // 2 : (h + 1) * T // 2], v_half[h][:], ACT.Copy)
-            summed = tile([P, I], F32, f"summed{h}", f"v_half{h}")
-            z = tile([P, 1], F32, f"z{h}")
-            nc.scalar.activation(summed[:], part[:], ACT.Copy, accum_out=z[:])
-            sums.append(z)
+            nc.vector.tensor_tensor(part[:], roots[h][:].indirect(link_list[:]), exps[h][:], ALU.mult)
             parts.append(part)
+        v0_codes = tile([P, P], U32, "v0_codes")
+        v0_scales = tile([P, P], U8, "v0_scales")
+        quantize(v0_codes[:], v0_scales[:], v0_turned[:])
 
-        gather_values(CAST_PLANE)
+        def row_sum(h, tag):
+            summed = tile([P, I], F32, f"summed{h}", tag)
+            total = tile([P, 1], F32, f"total{h}")
+            nc.scalar.activation(summed[:], parts[h][:], ACT.Copy, accum_out=total[:])
+            return total
 
-        def inverse_sum(h, tag):
-            inverse = tile([P, 1], F32, f"inverse{h}", tag)
-            nc.vector.reciprocal(inverse[:], sums[h][:])
-            return inverse
+        cast_piece(1)
+        totals = [row_sum(0, None), row_sum(1, "v_piece1")]
+        cast_piece(2)
+        listed_v1 = gather_values(1)
 
-        def weights(h, inverse, tag):
-            w_bf = tile([P, 2, P, 2], BF16, f"w_bf{h}", tag)
-            w_turned = ps.tile([P, 2, P], F32, name=f"w_turned{h}", tag=f"scores{h}")
+        mid_turned = tile([P, 4 * I], BF16, "mid_turned", "v1_bf")
+        for h in range(HALVES):
+            inverse = tile([P, 1], F32, f"inverse{h}")
+            nc.vector.reciprocal(inverse[:], totals[h][:])
+            w_bf = tile([P, 2, P, 2], BF16, f"w_bf{h}")
+            w_turned = bank([P, 2, P], f"w_turned{h}", f"scores{h}")
             for u in range(2):
                 nc.vector.scalar_tensor_tensor(
                     w_bf[:, u], parts[h][:].rearrange("p (s u e) -> p u s e", u=2, e=2)[:, u],
-                    inverse[:], os_rows[:, 2 * u : 2 * u + 2, :].rearrange("p e s -> p s e"), ALU.mult, ALU.mult,
+                    inverse[:], factor_rows[:, 2 * u : 2 * u + 2, :].rearrange("p e s -> p s e"), ALU.mult, ALU.mult,
                 )
                 nc.tensor.transpose(w_turned[:, u, :], w_bf[:, u].rearrange("p s e -> p (s e)").bitcast(F32), ident[:])
-            nc.scalar.copy(
-                wt_bf[h].bitcast(F32).rearrange("p (c u) -> p c u", u=2),
-                w_turned[:].rearrange("p u c -> p c u"),
-            )
+            copy_turned(mid_turned[:, h * I : (h + 1) * I], w_turned)
 
-        gather_values(2)
-        inverse = inverse_sum(0, "v_raw2")
-        (v0,) = quantize(turned_a[:], 1, "mx_a", "z0")
-        weights(0, inverse, None)
-        inverse = inverse_sum(1, "part0")
-        gather_values(3)
-        weights(1, inverse, "v_raw3")
-        v1, w0 = quantize(turned_b[:, : 2 * I], 2, "mx_b", "part1")
-        v2, v3 = quantize(turned_b[:, 2 * I :], 2, "mx_c")
-        (w1,) = quantize(turned_d[:], 1, "mx_d")
+        turn_values(1, listed_v1, mid_turned[:, 2 * I : 3 * I])
+        turn_values(2, gather_values(2), mid_turned[:, 3 * I :])
+        v3_turned = tile([P, I], BF16, "v3_turned")
+        turn_values(3, gather_values(3), v3_turned[:])
+
+        mid_codes = tile([P, 4 * P], U32, "mid_codes", "v_raw3")
+        mid_scales = tile([P, 4 * P], U8, "mid_scales")
+        for j in range(2):
+            cols = slice(2 * j * P, 2 * (j + 1) * P)
+            quantize(mid_codes[:, cols], mid_scales[:, cols], mid_turned[:, 2 * j * I : 2 * (j + 1) * I])
+        v3_codes = tile([P, P], U32, "v3_codes")
+        v3_scales = tile([P, P], U8, "v3_scales")
+        quantize(v3_codes[:], v3_scales[:], v3_turned[:])
+        v_mx = [
+            (v0_codes[:], v0_scales[:]),
+            (mid_codes[:, 2 * P : 3 * P], mid_scales[:, 2 * P : 3 * P]),
+            (mid_codes[:, 3 * P :], mid_scales[:, 3 * P :]),
+            (v3_codes[:], v3_scales[:]),
+        ]
 
         out_rows = out_0.rearrange("(p t) q -> p t q", t=PACK)
-        y_bf = tile([P, Q, PACK], BF16, "y_bf")
+        staged = tile([P, PACK, Q], F32, "staged")
+
+        def product(name, tag, planes, cols, copy):
+            result = bank([P, len(planes), cols.stop - cols.start], name, tag)
+            for j, t in enumerate(planes):
+                nc.tensor.matmul_mx(
+                    result[:, j, :], lhsT=v_mx[t][0].bitcast(FP8X4), lhsT_scale=v_mx[t][1],
+                    rhs=mid_codes[:, cols].bitcast(FP8X4), rhs_scale=mid_scales[:, cols], start=True, stop=True,
+                )
+            copy(staged[:, planes[0] : planes[-1] + 1, cols], result[:])
+
+        product("result01", None, (0, 1), slice(0, Q), nc.scalar.copy)
+        product("result2", "factor_rows", (2,), slice(0, Q), nc.vector.tensor_copy)
+        product("result3a", None, (3,), halves[1], nc.vector.tensor_copy)
+        product("result3b", "scores0", (3,), halves[0], nc.scalar.copy)
+        for j in range(2):
+            nc.sync.dma_start(out_rows[:, 2 * j : 2 * j + 2, :], staged[:, 2 * j : 2 * j + 2, :])
+
         y_codes = tile([P, Q], I32, "y_codes")
         y_scales = tile([P, Q], U8, "y_scales")
-        for h, (w_codes, w_scales) in enumerate((w0, w1)):
-            cols = slice(h * P, (h + 1) * P)
-            staged = tile([P, PACK, P], F32, f"staged{h}")
-            for j, pair in enumerate(((v0, v1), (v2, v3))):
-                result = ps.tile([P, 2, P], F32, name=f"result{h}_{j}", tag=(f"result{h}", f"v_turned{h + 1}")[j])
-                for t, (v_codes, v_scales) in enumerate(pair):
-                    nc.tensor.matmul_mx(
-                        result[:, t, :], lhsT=v_codes, lhsT_scale=v_scales, rhs=w_codes, rhs_scale=w_scales,
-                        start=True, stop=True,
-                    )
-                nc.scalar.copy(staged[:, 2 * j : 2 * j + 2, :], result[:])
-            (nc.sync, nc.scalar)[h].dma_start(out_rows[:, :, cols], staged[:])
-            nc.vector.tensor_copy(
-                y_bf[:, cols, :].rearrange("p (c i) t -> p c t i", i=4), staged[:].rearrange("p t (c i) -> p c t i", i=4)
-            )
+        y_bf = [tile([P, P * PACK], BF16, f"y_bf{h}") for h in range(HALVES)]
+        interleave(nc.vector.tensor_copy, y_bf[0][:], staged[:, :, halves[0]])
+        interleave(nc.scalar.copy, y_bf[1][:], staged[:, :, halves[1]])
         for h in range(HALVES):
-            cols = slice(h * P, (h + 1) * P)
-            nc.vector.quantize_mx(
-                y_codes[:, cols].bitcast(FP8X4), y_scales[:, cols], y_bf[:, cols, :].rearrange("p c t -> p (c t)")
-            )
+            quantize(y_codes[:, halves[h]], y_scales[:, halves[h]], y_bf[h][:])
         nc.sync.dma_start(out_1[0].rearrange("p c r -> p (c r)").bitcast(I32), y_codes[:])
         for quad in range(4):
             (nc.scalar, nc.sync)[quad % 2].dma_start(

from contextlib import ExitStack

import concourse.mybir as mybir
from concourse.masks import make_identity

D, E, T, I, Q = 512, 512, 2048, 512, 256
FLOPS = 2 * Q * I * D + 2 * E * Q * I

F32 = mybir.dt.float32
BF16 = mybir.dt.bfloat16
I32 = mybir.dt.int32
U32 = mybir.dt.uint32
U16 = mybir.dt.uint16
U8 = mybir.dt.uint8
FP8X4 = mybir.dt.float8_e4m3fn_x4
ALU = mybir.AluOpType
ACT = mybir.ActivationFunctionType

P = 128
PACK = 4
HALVES = Q // P
SPARE = 16
CAST_CUTS = (0, 768, 1408, T)


def tile_attend_linkedproduct_pl_kernel(
    tc, query, keys_words, keys_scales, slot_factor, vals, offs2, offs, out_0, out_1, out_2
):
    nc = tc.nc
    with ExitStack() as ctx:
        sb = ctx.enter_context(tc.tile_pool(name="sb", bufs=1))
        ps = ctx.enter_context(tc.psum_pool(name="ps", bufs=1))

        def tile(shape, dtype, name, tag=None):
            return sb.tile(shape, dtype, name=name, tag=tag or name, align_bytes=64)

        def bank(shape, name, tag=None):
            return ps.tile(shape, F32, name=name, tag=tag or name)

        slot_list = tile([P, I // 16], U16, "slot_list")
        link_list = tile([P, I // 16], U16, "link_list")
        key_scales = tile([P, T], U8, "key_scales")
        key_words = tile([P, T], I32, "key_words")
        q_raw = tile([P, PACK, Q], F32, "q_raw")
        factor_cols = tile([P, PACK], F32, "factor_cols")
        v_raw = {t: tile([P, T], F32, f"v_raw{t}") for t in (0, 2, 3)}
        pieces = [slice(CAST_CUTS[j], CAST_CUTS[j + 1]) for j in range(3)]
        v_piece = [tile([P, cols.stop - cols.start], F32, f"v_piece{j}") for j, cols in enumerate(pieces)]

        scale_words = key_scales[:].bitcast(I32)
        nc.vector.memset(scale_words, 0)
        v_planes = vals.rearrange("(p t) n -> t p n", t=PACK)
        nc.sync.dma_start(key_words[:], keys_words[0].rearrange("p n r -> p (n r)").bitcast(I32))
        nc.sync.dma_start(slot_list[:], offs)
        for r in range(4):
            nc.sync.dma_start(scale_words[r:P:32, :], keys_scales[0].bitcast(I32)[r:16:4, :])
        nc.sync.dma_start(q_raw[:], query.rearrange("(p t) q -> p t q", t=PACK))
        nc.sync.dma_start(v_piece[0][:], v_planes[1][:, pieces[0]])
        nc.sync.dma_start(v_raw[0][:], v_planes[0])
        nc.sync.dma_start(link_list[:], offs2)
        nc.sync.dma_start(factor_cols[:], slot_factor.rearrange("o (p t) -> (o p) t", t=PACK))
        nc.sync.dma_start(v_piece[1][:], v_planes[1][:, pieces[1]])
        nc.sync.dma_start(v_raw[2][:], v_planes[2])
        nc.sync.dma_start(v_piece[2][:], v_planes[1][:, pieces[2]])
        nc.sync.dma_start(v_raw[3][:], v_planes[3])

        ident = tile([P, P], F32, "ident")
        make_identity(nc, ident[:])
        zeros = tile([P, SPARE], F32, "zeros")
        nc.gpsimd.memset(zeros[:], 0.0)
        roots = [tile([P, I + SPARE], F32, f"roots{h}") for h in range(HALVES)]
        for h in range(HALVES):
            nc.scalar.activation(roots[h][:, I:], zeros[:], ACT.Exp)

        listed_words = tile([P, I], U32, "listed_words")
        listed_scales = tile([P, I], U8, "listed_scales")
        nc.vector.tensor_copy(listed_words[:], key_words[:].bitcast(U32).indirect(slot_list[:]))
        nc.vector.tensor_copy(listed_scales[:], key_scales[:].indirect(slot_list[:]))

        def quantize(codes, scales, values):
            nc.vector.quantize_mx(codes.bitcast(FP8X4), scales, values)

        def interleave(copy, side_by_side, planes):
            copy(
                side_by_side.rearrange("p (c i t) -> p c t i", i=4, t=PACK),
                planes.rearrange("p t (c i) -> p c t i", i=4),
            )

        q_codes = tile([P, Q], U32, "q_codes")
        q_scales = tile([P, Q], U8, "q_scales")
        halves = [slice(h * P, (h + 1) * P) for h in range(HALVES)]
        for h in range(HALVES):
            q_bf = tile([P, P * PACK], BF16, f"q_bf{h}")
            interleave(nc.scalar.copy, q_bf[:], q_raw[:, :, halves[h]])
            quantize(q_codes[:, halves[h]], q_scales[:, halves[h]], q_bf[:])

        v1_bf = tile([P, T], BF16, "v1_bf")

        def cast_piece(j):
            nc.scalar.activation(v1_bf[:, pieces[j]], v_piece[j][:], ACT.Copy)

        cast_piece(0)

        exps = []
        for h in range(HALVES):
            scores = bank([P, I], f"scores{h}")
            nc.tensor.matmul_mx(
                scores[:], lhsT=q_codes[:, halves[h]].bitcast(FP8X4), lhsT_scale=q_scales[:, halves[h]],
                rhs=listed_words[:].bitcast(FP8X4), rhs_scale=listed_scales[:], start=True, stop=True,
            )
            neg_half = tile([P, I], F32, f"neg_half{h}")
            shift = tile([P, 1], F32, f"shift{h}")
            nc.vector.tensor_scalar(neg_half[:], scores[:], -0.5, None, ALU.mult, ALU.min, accum_out=shift[:])
            nc.scalar.activation(roots[h][:, :I], neg_half[:], ACT.Exp, bias=shift[:], scale=-1.0)
            exp_h = tile([P, I], F32, f"exps{h}")
            nc.scalar.activation(exp_h[:], roots[h][:, :I], ACT.Square)
            exps.append(exp_h)

        factor_rows = bank([P, PACK, P], "factor_rows")
        for t in range(PACK):
            nc.tensor.transpose(factor_rows[:, t, :], factor_cols[:, t : t + 1].to_broadcast([P, P]), ident[:])

        def copy_turned(side_by_side, turned):
            nc.scalar.copy(
                side_by_side.bitcast(F32).rearrange("p (c u) -> p c u", u=2), turned[:].rearrange("p u c -> p c u")
            )

        def gather_values(t):
            listed = tile([P, I], BF16, f"listed_v{t}")
            if t == 1:
                nc.scalar.activation(listed[:], v1_bf[:].indirect(slot_list[:]), ACT.Copy)
            else:
                nc.vector.tensor_copy(listed[:], v_raw[t][:].indirect(slot_list[:]))
            return listed

        def turn_values(t, listed, side_by_side):
            turned = bank([P, 2, P], f"v_turned{t}", f"v_turned{t % 3}")
            pairs = listed[:].bitcast(F32)
            for u in range(2):
                nc.tensor.transpose(turned[:, u, :], pairs[:, u::2], ident[:])
            copy_turned(side_by_side, turned)

        v0_turned = tile([P, I], BF16, "v0_turned")
        turn_values(0, gather_values(0), v0_turned[:])

        parts = []
        for h in range(HALVES):
            part = tile([P, I], F32, f"part{h}")
            nc.vector.tensor_tensor(part[:], roots[h][:].indirect(link_list[:]), exps[h][:], ALU.mult)
            parts.append(part)
        v0_codes = tile([P, P], U32, "v0_codes")
        v0_scales = tile([P, P], U8, "v0_scales")
        quantize(v0_codes[:], v0_scales[:], v0_turned[:])

        def row_sum(h, tag):
            summed = tile([P, I], F32, f"summed{h}", tag)
            total = tile([P, 1], F32, f"total{h}")
            nc.scalar.activation(summed[:], parts[h][:], ACT.Copy, accum_out=total[:])
            return total

        cast_piece(1)
        totals = [row_sum(0, None), row_sum(1, "v_piece1")]
        cast_piece(2)
        listed_v1 = gather_values(1)

        mid_turned = tile([P, 4 * I], BF16, "mid_turned", "v1_bf")
        for h in range(HALVES):
            inverse = tile([P, 1], F32, f"inverse{h}")
            nc.vector.reciprocal(inverse[:], totals[h][:])
            w_bf = tile([P, 2, P, 2], BF16, f"w_bf{h}")
            w_turned = bank([P, 2, P], f"w_turned{h}", f"scores{h}")
            for u in range(2):
                nc.vector.scalar_tensor_tensor(
                    w_bf[:, u], parts[h][:].rearrange("p (s u e) -> p u s e", u=2, e=2)[:, u],
                    inverse[:], factor_rows[:, 2 * u : 2 * u + 2, :].rearrange("p e s -> p s e"), ALU.mult, ALU.mult,
                )
                nc.tensor.transpose(w_turned[:, u, :], w_bf[:, u].rearrange("p s e -> p (s e)").bitcast(F32), ident[:])
            copy_turned(mid_turned[:, h * I : (h + 1) * I], w_turned)

        turn_values(1, listed_v1, mid_turned[:, 2 * I : 3 * I])
        turn_values(2, gather_values(2), mid_turned[:, 3 * I :])
        v3_turned = tile([P, I], BF16, "v3_turned")
        turn_values(3, gather_values(3), v3_turned[:])

        mid_codes = tile([P, 4 * P], U32, "mid_codes", "v_raw3")
        mid_scales = tile([P, 4 * P], U8, "mid_scales")
        for j in range(2):
            cols = slice(2 * j * P, 2 * (j + 1) * P)
            quantize(mid_codes[:, cols], mid_scales[:, cols], mid_turned[:, 2 * j * I : 2 * (j + 1) * I])
        v3_codes = tile([P, P], U32, "v3_codes")
        v3_scales = tile([P, P], U8, "v3_scales")
        quantize(v3_codes[:], v3_scales[:], v3_turned[:])
        v_mx = [
            (v0_codes[:], v0_scales[:]),
            (mid_codes[:, 2 * P : 3 * P], mid_scales[:, 2 * P : 3 * P]),
            (mid_codes[:, 3 * P :], mid_scales[:, 3 * P :]),
            (v3_codes[:], v3_scales[:]),
        ]

        out_rows = out_0.rearrange("(p t) q -> p t q", t=PACK)
        staged = tile([P, PACK, Q], F32, "staged")

        def product(name, tag, planes, cols, copy):
            result = bank([P, len(planes), cols.stop - cols.start], name, tag)
            for j, t in enumerate(planes):
                nc.tensor.matmul_mx(
                    result[:, j, :], lhsT=v_mx[t][0].bitcast(FP8X4), lhsT_scale=v_mx[t][1],
                    rhs=mid_codes[:, cols].bitcast(FP8X4), rhs_scale=mid_scales[:, cols], start=True, stop=True,
                )
            copy(staged[:, planes[0] : planes[-1] + 1, cols], result[:])

        product("result01", None, (0, 1), slice(0, Q), nc.scalar.copy)
        product("result2", "factor_rows", (2,), slice(0, Q), nc.vector.tensor_copy)
        product("result3a", None, (3,), halves[1], nc.vector.tensor_copy)
        product("result3b", "scores0", (3,), halves[0], nc.scalar.copy)
        for j in range(2):
            nc.sync.dma_start(out_rows[:, 2 * j : 2 * j + 2, :], staged[:, 2 * j : 2 * j + 2, :])

        y_codes = tile([P, Q], I32, "y_codes")
        y_scales = tile([P, Q], U8, "y_scales")
        y_bf = [tile([P, P * PACK], BF16, f"y_bf{h}") for h in range(HALVES)]
        interleave(nc.vector.tensor_copy, y_bf[0][:], staged[:, :, halves[0]])
        interleave(nc.scalar.copy, y_bf[1][:], staged[:, :, halves[1]])
        for h in range(HALVES):
            quantize(y_codes[:, halves[h]], y_scales[:, halves[h]], y_bf[h][:])
        nc.sync.dma_start(out_1[0].rearrange("p c r -> p (c r)").bitcast(I32), y_codes[:])
        for quad in range(4):
            (nc.scalar, nc.sync)[quad % 2].dma_start(
                out_2[0, 4 * quad : 4 * quad + 4, :].bitcast(I32),
                y_scales[32 * quad : 32 * quad + 4, :].bitcast(I32),
            )
